import numpy as np, ml_dtypes
CORES = [21,29,37,45,53,61,69,77,85]
N = 9
TK = 32
def setup_inputs(rng):
    return {"c": rng.standard_normal((N, 128, 128), dtype=np.float32).astype(ml_dtypes.bfloat16), "x": rng.standard_normal((N, 128, TK), dtype=np.float32).astype(ml_dtypes.bfloat16)}
def setup_inputs_big(rng):
    d = setup_inputs(rng)
    for k in ("c", "x"): d[k] = (d[k].astype(np.float32) * 1024.0).astype(d[k].dtype)
    return d
def setup_inputs_small(rng):
    d = setup_inputs(rng)
    for k in ("c", "x"): d[k] = (d[k].astype(np.float32) * (1 / 1024.0)).astype(d[k].dtype)
    return d
def setup_inputs_apart(rng):
    d = setup_inputs(rng)
    f = (10.0 ** rng.permutation(np.linspace(-1.5, 1.5, N))).astype(np.float32).reshape(N, 1, 1)
    for k in ("c", "x"): d[k] = (d[k].astype(np.float32) * f).astype(d[k].dtype)
    return d
def reference(c, x):
    C, X = c.astype(np.float64), x.astype(np.float64)
    y = np.zeros((N, 128, TK))
    for r in range(N):
        for j in range(N):
            y[r] += C[(r - j) % N].T @ X[j]
    return {"y": y.astype(ml_dtypes.bfloat16 if x.dtype != np.float64 else np.float64)}

@@ -1,0 +1,155 @@
+from concourse.bass import DstId, RemoteDMATransfer
+
+SIM_CORES = 96
+N = 9
+CW = 128
+XW = 32
+W = CW + XW
+
+SIDE = 0
+
+SCRATCH = {
+    "blk": ("dram", [128, W], "bfloat16"),
+    "rel": ("dram", [128, W], "bfloat16"),
+    "land": ("sbuf", [128, N * W], "bfloat16"),
+    "ysb": ("sbuf", [128, XW], "bfloat16"),
+    "ps": ("psum", [128, XW], "float32"),
+}
+SEMAPHORES = ["ld", "own", "rel", "sent", "mm", "cp", "st"] + ["a%d" % k for k in range(N)]
+
+
+def _bits(m):
+    return bin(m).count("1")
+
+
+def _plan(T, topo):
+    R = list(T.cores)
+    n = len(R)
+    group = set(R)
+    on_chip = {}
+    for c in range(SIM_CORES):
+        on_chip.setdefault(topo.chip(c), []).append(c)
+    busy = set(topo.chip(c) for c in R)
+    reach = [[r for r in range(n) if r == k or topo.may_write(R[k], R[r])] for k in range(n)]
+    pos = [reach[k].index(k) for k in range(n)]
+
+    def by_turns(cores):
+        lanes = {}
+        for c in cores:
+            lanes.setdefault(topo.die(c), []).append(c)
+        lanes = [lanes[d] for d in sorted(lanes)]
+        out = []
+        for i in range(max(len(l) for l in lanes)):
+            out += [l[i] for l in lanes if i < len(l)]
+        return out
+
+    def ports(chip, dst):
+        return by_turns([c for c in on_chip[chip] if c not in group and topo.may_write(c, dst)])
+
+    direct, near, far = {}, {}, {}
+    for k in range(n):
+        direct[k], near[k], far[k] = [], [], []
+        home = topo.chip(R[k])
+        m = len(reach[k])
+        used = set()
+        for r in range(n):
+            if r == k or topo.may_write(R[k], R[r]):
+                continue
+            idle = [ch for ch in on_chip if ch not in busy and topo.mates(ch, topo.chip(R[r]))
+                    and topo.same_plane(ch, home)]
+            if idle:
+                p = ports(idle[0], R[r])
+                far[k].append((p[pos[k] % len(p)], r))
+            else:
+                p = ports(home, R[r])
+                near[k].append((p[(pos[k] + pos[r]) % len(p)], r))
+                used.update(p)
+        near[k].sort(key=lambda cr: ports(home, R[cr[1]]).index(cr[0]))
+        same = sorted((r for r in reach[k] if r != k), key=lambda r: (pos[r] - pos[k]) % m)
+        spare = [c for c in on_chip[home] if c not in group and c not in used]
+        spare.sort(key=lambda c: topo.die(c) != topo.die(R[k]))
+        ns = min(SIDE, len(spare), len(same))
+        direct[k] = same[:len(same) - ns]
+        near[k] += list(zip(spare, same[len(same) - ns:]))
+    return R, direct, near, far
+
+
+def _dst(topo, core):
+    rid, pid, _ = topo.addr(core)
+    return DstId(rid=rid, pnc=pid)
+
+
+def _slot(T, k):
+    return T.land[:, k * W:(k + 1) * W]
+
+
+def rank_program(g, core, T, topo):
+    R, direct, near, far = _plan(T, topo)
+    n = len(R)
+    rank = T.rank_of(core)
+
+    if rank is None:
+        for k in range(n):
+            for table, sem, src in ((near[k], T.sem.rel, T.rel[:]), (far[k], T.sem["a%d" % k], _slot(T, k))):
+                for c, r in table:
+                    if c != core:
+                        continue
+                    up = topo.mask(R[k], core)
+                    if table is near[k]:
+                        up = up & ~topo.mask(R[k], R[direct[k][0]])
+                    m = topo.mask(core, R[r])
+                    rid, pid, _ = topo.addr(R[r])
+                    g.wait_ge(sem, _bits(up))
+                    g.remote_dma(out_ap=_slot(T, k), in_ap=src, remote_sem=T.sem["a%d" % k], local_sem=T.sem.sent,
+                                 pid=pid, routing_id=rid, dma_engine_mask=m)
+                    g.wait_ge(T.sem.sent, _bits(m))
+        return
+
+    k = rank
+    g.sync.dma_start(T.blk[:, 0:CW], T.c[:]).then_inc(T.sem.ld, 16)
+    g.scalar.dma_start(T.blk[:, CW:W], T.x[:]).then_inc(T.sem.ld, 16)
+    g.sync.dma_start(T.land[:, k * W:k * W + CW], T.c[:]).then_inc(T.sem.own, 16)
+    g.scalar.dma_start(T.land[:, k * W + CW:(k + 1) * W], T.x[:]).then_inc(T.sem.own, 16)
+
+    off = topo.mask(core, R[direct[k][0]])
+    stay = topo.mask(core, near[k][0][0]) & ~off
+    g.wait_ge(T.sem.ld, 32)
+    g.remote_dma_fused([RemoteDMATransfer(
+        dst_ids=[_dst(topo, c) for c, _ in near[k]], dma_engine_mask=stay, remote_sem=T.sem.rel,
+        srcs=[T.blk[:]], dsts=[T.rel[:] for _ in near[k]])], local_sem=T.sem.sent)
+    outs = [c for c, _ in far[k]] + [R[r] for r in direct[k]]
+    g.remote_dma_fused([RemoteDMATransfer(
+        dst_ids=[_dst(topo, c) for c in outs], dma_engine_mask=off, remote_sem=T.sem["a%d" % k],
+        srcs=[T.blk[:]], dsts=[_slot(T, k) for _ in outs])], local_sem=T.sem.sent)
+
+    due, cnt = {k: 0}, {}
+    for s in range(n):
+        if s == k:
+            continue
+        if k in direct[s]:
+            due[s] = 1 + len(far[s]) + direct[s].index(k)
+            cnt[s] = _bits(topo.mask(R[s], core))
+        else:
+            hops = near[s] + far[s]
+            i = [r for _, r in hops].index(k)
+            due[s] = 100 + i
+            cnt[s] = _bits(topo.mask(hops[i][0], core))
+
+    order = sorted(range(n), key=lambda a: (max(due[a], due[(k - a) % n]), a))
+    seen = set([k])
+    g.tensor.wait_ge(T.sem.own, 32)
+    for i, a in enumerate(order):
+        j = (k - a) % n
+        for s in sorted((a, j), key=lambda s: due[s]):
+            if s not in seen:
+                seen.add(s)
+                g.tensor.wait_ge(T.sem["a%d" % s], cnt[s])
+        g.tensor.matmul(T.ps[:], T.land[:, a * W:a * W + CW], T.land[:, j * W + CW:(j + 1) * W],
+                        i == 0, i == n - 1).then_inc(T.sem.mm, 1)
+
+    g.vector.wait_ge(T.sem.mm, n)
+    g.vector.tensor_copy(T.ysb[:], T.ps[:]).then_inc(T.sem.cp, 1)
+    g.sync.wait_ge(T.sem.cp, 1)
+    g.sync.dma_start(T.y[:], T.ysb[:]).then_inc(T.sem.st, 16)
+    g.sync.wait_ge(T.sem.st, 16)
+    g.wait_ge(T.sem.sent, _bits(stay) + _bits(off))

@@ -6,8 +6,6 @@ CW = 128
 XW = 32
 W = CW + XW
 
-SIDE = 0
-
 SCRATCH = {
     "blk": ("dram", [128, W], "bfloat16"),
     "rel": ("dram", [128, W], "bfloat16"),
@@ -26,52 +24,35 @@ def _plan(T, topo):
     R = list(T.cores)
     n = len(R)
     group = set(R)
-    on_chip = {}
-    for c in range(SIM_CORES):
-        on_chip.setdefault(topo.chip(c), []).append(c)
-    busy = set(topo.chip(c) for c in R)
     reach = [[r for r in range(n) if r == k or topo.may_write(R[k], R[r])] for k in range(n)]
     pos = [reach[k].index(k) for k in range(n)]
 
-    def by_turns(cores):
+    def ports(chip, dst):
         lanes = {}
-        for c in cores:
-            lanes.setdefault(topo.die(c), []).append(c)
+        for c in range(SIM_CORES):
+            if topo.chip(c) == chip and c not in group and topo.may_write(c, dst):
+                lanes.setdefault(topo.die(c), []).append(c)
         lanes = [lanes[d] for d in sorted(lanes)]
         out = []
         for i in range(max(len(l) for l in lanes)):
             out += [l[i] for l in lanes if i < len(l)]
         return out
 
-    def ports(chip, dst):
-        return by_turns([c for c in on_chip[chip] if c not in group and topo.may_write(c, dst)])
-
-    direct, near, far = {}, {}, {}
+    direct, relay, feed, off = {}, {}, {}, {}
     for k in range(n):
-        direct[k], near[k], far[k] = [], [], []
         home = topo.chip(R[k])
-        m = len(reach[k])
-        used = set()
+        work = {}
         for r in range(n):
             if r == k or topo.may_write(R[k], R[r]):
                 continue
-            idle = [ch for ch in on_chip if ch not in busy and topo.mates(ch, topo.chip(R[r]))
-                    and topo.same_plane(ch, home)]
-            if idle:
-                p = ports(idle[0], R[r])
-                far[k].append((p[pos[k] % len(p)], r))
-            else:
-                p = ports(home, R[r])
-                near[k].append((p[(pos[k] + pos[r]) % len(p)], r))
-                used.update(p)
-        near[k].sort(key=lambda cr: ports(home, R[cr[1]]).index(cr[0]))
-        same = sorted((r for r in reach[k] if r != k), key=lambda r: (pos[r] - pos[k]) % m)
-        spare = [c for c in on_chip[home] if c not in group and c not in used]
-        spare.sort(key=lambda c: topo.die(c) != topo.die(R[k]))
-        ns = min(SIDE, len(spare), len(same))
-        direct[k] = same[:len(same) - ns]
-        near[k] += list(zip(spare, same[len(same) - ns:]))
-    return R, direct, near, far
+            p = ports(home, R[r])
+            i = (pos[k] + pos[r]) % len(p)
+            work.setdefault((i, p[i]), []).append(r)
+        relay[k] = [(c, work[(i, c)]) for i, c in sorted(work, key=lambda ic: (-len(work[ic]), ic[0]))]
+        direct[k] = sorted((r for r in reach[k] if r != k), key=lambda r: (pos[r] - pos[k]) % len(reach[k]))
+        off[k] = topo.mask(R[k], R[direct[k][0]])
+        feed[k] = topo.mask(R[k], relay[k][0][0]) & ~off[k]
+    return R, direct, relay, feed, off
 
 
 def _dst(topo, core):
@@ -84,25 +65,21 @@ def _slot(T, k):
 
 
 def rank_program(g, core, T, topo):
-    R, direct, near, far = _plan(T, topo)
+    R, direct, relay, feed, off = _plan(T, topo)
     n = len(R)
     rank = T.rank_of(core)
 
     if rank is None:
         for k in range(n):
-            for table, sem, src in ((near[k], T.sem.rel, T.rel[:]), (far[k], T.sem["a%d" % k], _slot(T, k))):
-                for c, r in table:
-                    if c != core:
-                        continue
-                    up = topo.mask(R[k], core)
-                    if table is near[k]:
-                        up = up & ~topo.mask(R[k], R[direct[k][0]])
-                    m = topo.mask(core, R[r])
-                    rid, pid, _ = topo.addr(R[r])
-                    g.wait_ge(sem, _bits(up))
-                    g.remote_dma(out_ap=_slot(T, k), in_ap=src, remote_sem=T.sem["a%d" % k], local_sem=T.sem.sent,
-                                 pid=pid, routing_id=rid, dma_engine_mask=m)
-                    g.wait_ge(T.sem.sent, _bits(m))
+            for c, rs in relay[k]:
+                if c != core:
+                    continue
+                m = topo.mask(core, R[rs[0]])
+                g.wait_ge(T.sem.rel, _bits(feed[k]))
+                g.remote_dma_fused([RemoteDMATransfer(
+                    dst_ids=[_dst(topo, R[r]) for r in rs], dma_engine_mask=m, remote_sem=T.sem["a%d" % k],
+                    srcs=[T.rel[:]], dsts=[_slot(T, k) for _ in rs])], local_sem=T.sem.sent)
+                g.wait_ge(T.sem.sent, _bits(m))
         return
 
     k = rank
@@ -111,29 +88,26 @@ def rank_program(g, core, T, topo):
     g.sync.dma_start(T.land[:, k * W:k * W + CW], T.c[:]).then_inc(T.sem.own, 16)
     g.scalar.dma_start(T.land[:, k * W + CW:(k + 1) * W], T.x[:]).then_inc(T.sem.own, 16)
 
-    off = topo.mask(core, R[direct[k][0]])
-    stay = topo.mask(core, near[k][0][0]) & ~off
     g.wait_ge(T.sem.ld, 32)
     g.remote_dma_fused([RemoteDMATransfer(
-        dst_ids=[_dst(topo, c) for c, _ in near[k]], dma_engine_mask=stay, remote_sem=T.sem.rel,
-        srcs=[T.blk[:]], dsts=[T.rel[:] for _ in near[k]])], local_sem=T.sem.sent)
-    outs = [c for c, _ in far[k]] + [R[r] for r in direct[k]]
+        dst_ids=[_dst(topo, c) for c, _ in relay[k]], dma_engine_mask=feed[k], remote_sem=T.sem.rel,
+        srcs=[T.blk[:]], dsts=[T.rel[:] for _ in relay[k]])], local_sem=T.sem.sent)
     g.remote_dma_fused([RemoteDMATransfer(
-        dst_ids=[_dst(topo, c) for c in outs], dma_engine_mask=off, remote_sem=T.sem["a%d" % k],
-        srcs=[T.blk[:]], dsts=[_slot(T, k) for _ in outs])], local_sem=T.sem.sent)
+        dst_ids=[_dst(topo, R[r]) for r in direct[k]], dma_engine_mask=off[k], remote_sem=T.sem["a%d" % k],
+        srcs=[T.blk[:]], dsts=[_slot(T, k) for _ in direct[k]])], local_sem=T.sem.sent)
 
     due, cnt = {k: 0}, {}
     for s in range(n):
         if s == k:
             continue
         if k in direct[s]:
-            due[s] = 1 + len(far[s]) + direct[s].index(k)
-            cnt[s] = _bits(topo.mask(R[s], core))
+            due[s] = 1 + direct[s].index(k)
+            cnt[s] = _bits(off[s])
         else:
-            hops = near[s] + far[s]
-            i = [r for _, r in hops].index(k)
-            due[s] = 100 + i
-            cnt[s] = _bits(topo.mask(hops[i][0], core))
+            for i, (c, rs) in enumerate(relay[s]):
+                if k in rs:
+                    due[s] = 100 + i + 4 * rs.index(k)
+                    cnt[s] = _bits(topo.mask(c, core))
 
     order = sorted(range(n), key=lambda a: (max(due[a], due[(k - a) % n]), a))
     seen = set([k])
@@ -152,4 +126,4 @@ def rank_program(g, core, T, topo):
     g.sync.wait_ge(T.sem.cp, 1)
     g.sync.dma_start(T.y[:], T.ysb[:]).then_inc(T.sem.st, 16)
     g.sync.wait_ge(T.sem.st, 16)
-    g.wait_ge(T.sem.sent, _bits(stay) + _bits(off))
+    g.wait_ge(T.sem.sent, _bits(feed[k]) + _bits(off[k]))

@@ -7,17 +7,42 @@ XW = 32
 W = CW + XW
 
 SCRATCH = {
+    "cb": ("dram", [128, CW], "bfloat16"),
+    "xb": ("dram", [128, XW], "bfloat16"),
     "blk": ("dram", [128, W], "bfloat16"),
-    "rel": ("dram", [128, W], "bfloat16"),
+    "relc": ("dram", [128, CW], "bfloat16"),
+    "relx": ("dram", [128, XW], "bfloat16"),
     "land": ("sbuf", [128, N * W], "bfloat16"),
     "ysb": ("sbuf", [128, XW], "bfloat16"),
     "ps": ("psum", [128, XW], "float32"),
 }
-SEMAPHORES = ["ld", "own", "rel", "sent", "mm", "cp", "st"] + ["a%d" % k for k in range(N)]
+SEMAPHORES = ["ldx", "ldc", "ld", "own", "rx", "rc", "sent", "mm", "cp", "st"] + ["a%d" % k for k in range(N)]
 
 
 def _bits(m):
     return bin(m).count("1")
+
+
+def _alternate(m):
+    out, i = [0, 0], 0
+    for b in range(m.bit_length()):
+        if m >> b & 1:
+            out[i] |= 1 << b
+            i = 1 - i
+    return out[0], out[1]
+
+
+def _route(topo, src, dst):
+    a, b, d = topo.chip(src), topo.chip(dst), topo.die(src)
+    if a == b:
+        return []
+    if topo.same_plane(a, b):
+        return [("out", a, d), ("in", b, d)]
+    links = [("mate", a, d)]
+    if not topo.mates(a, b):
+        m = [topo.chip(c) for c in range(SIM_CORES) if topo.mates(a, topo.chip(c))][0]
+        links += [("out", m, d), ("in", b, d)]
+    return links
 
 
 def _plan(T, topo):
@@ -26,32 +51,58 @@ def _plan(T, topo):
     group = set(R)
     reach = [[r for r in range(n) if r == k or topo.may_write(R[k], R[r])] for k in range(n)]
     pos = [reach[k].index(k) for k in range(n)]
+    far = [[r for r in range(n) if r not in reach[k]] for k in range(n)]
 
-    def ports(chip, dst):
-        lanes = {}
+    load = {}
+
+    def add(src, dst):
+        for l in _route(topo, src, dst):
+            load[l] = load.get(l, 0) + 1
+
+    for k in range(n):
+        for r in reach[k]:
+            if r != k:
+                add(R[k], R[r])
+
+    work = {}
+    for k in range(n):
+        work[k] = {}
         for c in range(SIM_CORES):
-            if topo.chip(c) == chip and c not in group and topo.may_write(c, dst):
-                lanes.setdefault(topo.die(c), []).append(c)
-        lanes = [lanes[d] for d in sorted(lanes)]
-        out = []
-        for i in range(max(len(l) for l in lanes)):
-            out += [l[i] for l in lanes if i < len(l)]
-        return out
+            if topo.chip(c) == topo.chip(R[k]) and c not in group and topo.may_write(c, R[far[k][0]]):
+                work[k][c] = []
+
+    todo = []
+    for k in range(n):
+        for r in far[k]:
+            todo.append((0 if topo.mates(topo.chip(R[k]), topo.chip(R[r])) else 1, (r - k) % n, k, r))
+    for _, _, k, r in sorted(todo):
+        best = None
+        for c in sorted(work[k]):
+            links = _route(topo, c, R[r])
+            sw = [load.get(l, 0) + 1 for l in links if l[0] != "mate"]
+            if sw:
+                busy = max(sw)
+            else:
+                busy = 0 if topo.die(c) == topo.die(R[k]) else n * n
+            key = (len(work[k][c]), busy, max(load.get(l, 0) + 1 for l in links), c)
+            if best is None or key < best:
+                best = key
+        work[k][best[3]].append(r)
+        add(best[3], R[r])
 
     direct, relay, feed, off = {}, {}, {}, {}
     for k in range(n):
-        home = topo.chip(R[k])
-        work = {}
-        for r in range(n):
-            if r == k or topo.may_write(R[k], R[r]):
-                continue
-            p = ports(home, R[r])
-            i = (pos[k] + pos[r]) % len(p)
-            work.setdefault((i, p[i]), []).append(r)
-        relay[k] = [(c, work[(i, c)]) for i, c in sorted(work, key=lambda ic: (-len(work[ic]), ic[0]))]
+        def rank_of_feed(c):
+            short = all(topo.mates(topo.chip(c), topo.chip(R[r])) for r in work[k][c])
+            return (-len(work[k][c]), short, topo.die(c) == topo.die(R[k]), c)
+        cores = [c for c in sorted(work[k], key=rank_of_feed) if work[k][c]]
+        xs = dict((c, work[k][c][:1]) for c in cores)
+        for c in cores:
+            xs[cores[-1]] = xs[cores[-1]] + work[k][c][1:]
+        relay[k] = [(c, work[k][c], xs[c]) for c in cores]
         direct[k] = sorted((r for r in reach[k] if r != k), key=lambda r: (pos[r] - pos[k]) % len(reach[k]))
         off[k] = topo.mask(R[k], R[direct[k][0]])
-        feed[k] = topo.mask(R[k], relay[k][0][0]) & ~off[k]
+        feed[k] = topo.mask(R[k], cores[0]) & ~off[k]
     return R, direct, relay, feed, off
 
 
@@ -64,6 +115,14 @@ def _slot(T, k):
     return T.land[:, k * W:(k + 1) * W]
 
 
+def _cpart(T, k):
+    return T.land[:, k * W:k * W + CW]
+
+
+def _xpart(T, k):
+    return T.land[:, k * W + CW:(k + 1) * W]
+
+
 def rank_program(g, core, T, topo):
     R, direct, relay, feed, off = _plan(T, topo)
     n = len(R)
@@ -71,27 +130,38 @@ def rank_program(g, core, T, topo):
 
     if rank is None:
         for k in range(n):
-            for c, rs in relay[k]:
+            for c, rs, xs in relay[k]:
                 if c != core:
                     continue
-                m = topo.mask(core, R[rs[0]])
-                g.wait_ge(T.sem.rel, _bits(feed[k]))
+                halves = _alternate(topo.mask(core, R[rs[0]]))
+                g.wait_ge(T.sem.rx, _bits(off[k]))
                 g.remote_dma_fused([RemoteDMATransfer(
-                    dst_ids=[_dst(topo, R[r]) for r in rs], dma_engine_mask=m, remote_sem=T.sem["a%d" % k],
-                    srcs=[T.rel[:]], dsts=[_slot(T, k) for _ in rs])], local_sem=T.sem.sent)
-                g.wait_ge(T.sem.sent, _bits(m))
+                    dst_ids=[_dst(topo, R[r]) for r in xs], dma_engine_mask=halves[1], remote_sem=T.sem["a%d" % k],
+                    srcs=[T.relx[:]], dsts=[_xpart(T, k) for _ in xs])], local_sem=T.sem.sent)
+                g.wait_ge(T.sem.rc, _bits(feed[k]))
+                g.remote_dma_fused([RemoteDMATransfer(
+                    dst_ids=[_dst(topo, R[r])], dma_engine_mask=halves[i], remote_sem=T.sem["a%d" % k],
+                    srcs=[T.relc[:]], dsts=[_cpart(T, k)]) for i, r in enumerate(rs)], local_sem=T.sem.sent)
+                g.wait_ge(T.sem.sent, _bits(halves[1]) + sum(_bits(halves[i]) for i in range(len(rs))))
         return
 
     k = rank
+    g.scalar.dma_start(T.xb[:], T.x[:]).then_inc(T.sem.ldx, 16)
+    g.sync.dma_start(T.cb[:], T.c[:]).then_inc(T.sem.ldc, 16)
     g.sync.dma_start(T.blk[:, 0:CW], T.c[:]).then_inc(T.sem.ld, 16)
     g.scalar.dma_start(T.blk[:, CW:W], T.x[:]).then_inc(T.sem.ld, 16)
-    g.sync.dma_start(T.land[:, k * W:k * W + CW], T.c[:]).then_inc(T.sem.own, 16)
-    g.scalar.dma_start(T.land[:, k * W + CW:(k + 1) * W], T.x[:]).then_inc(T.sem.own, 16)
+    g.sync.dma_start(_cpart(T, k), T.c[:]).then_inc(T.sem.own, 16)
+    g.scalar.dma_start(_xpart(T, k), T.x[:]).then_inc(T.sem.own, 16)
 
-    g.wait_ge(T.sem.ld, 32)
+    g.wait_ge(T.sem.ldx, 16)
     g.remote_dma_fused([RemoteDMATransfer(
-        dst_ids=[_dst(topo, c) for c, _ in relay[k]], dma_engine_mask=feed[k], remote_sem=T.sem.rel,
-        srcs=[T.blk[:]], dsts=[T.rel[:] for _ in relay[k]])], local_sem=T.sem.sent)
+        dst_ids=[_dst(topo, e[0]) for e in relay[k]], dma_engine_mask=off[k], remote_sem=T.sem.rx,
+        srcs=[T.xb[:]], dsts=[T.relx[:] for _ in relay[k]])], local_sem=T.sem.sent)
+    g.wait_ge(T.sem.ldc, 16)
+    g.remote_dma_fused([RemoteDMATransfer(
+        dst_ids=[_dst(topo, e[0]) for e in relay[k]], dma_engine_mask=feed[k], remote_sem=T.sem.rc,
+        srcs=[T.cb[:]], dsts=[T.relc[:] for _ in relay[k]])], local_sem=T.sem.sent)
+    g.wait_ge(T.sem.ld, 32)
     g.remote_dma_fused([RemoteDMATransfer(
         dst_ids=[_dst(topo, R[r]) for r in direct[k]], dma_engine_mask=off[k], remote_sem=T.sem["a%d" % k],
         srcs=[T.blk[:]], dsts=[_slot(T, k) for _ in direct[k]])], local_sem=T.sem.sent)
@@ -104,10 +174,14 @@ def rank_program(g, core, T, topo):
             due[s] = 1 + direct[s].index(k)
             cnt[s] = _bits(off[s])
         else:
-            for i, (c, rs) in enumerate(relay[s]):
+            cnt[s] = 0
+            for i, (c, rs, xs) in enumerate(relay[s]):
+                halves = _alternate(topo.mask(c, core))
                 if k in rs:
                     due[s] = 100 + i + 4 * rs.index(k)
-                    cnt[s] = _bits(topo.mask(c, core))
+                    cnt[s] += _bits(halves[rs.index(k)])
+                if k in xs:
+                    cnt[s] += _bits(halves[1])
 
     order = sorted(range(n), key=lambda a: (max(due[a], due[(k - a) % n]), a))
     seen = set([k])
@@ -118,12 +192,11 @@ def rank_program(g, core, T, topo):
             if s not in seen:
                 seen.add(s)
                 g.tensor.wait_ge(T.sem["a%d" % s], cnt[s])
-        g.tensor.matmul(T.ps[:], T.land[:, a * W:a * W + CW], T.land[:, j * W + CW:(j + 1) * W],
-                        i == 0, i == n - 1).then_inc(T.sem.mm, 1)
+        g.tensor.matmul(T.ps[:], _cpart(T, a), _xpart(T, j), i == 0, i == n - 1).then_inc(T.sem.mm, 1)
 
     g.vector.wait_ge(T.sem.mm, n)
     g.vector.tensor_copy(T.ysb[:], T.ps[:]).then_inc(T.sem.cp, 1)
     g.sync.wait_ge(T.sem.cp, 1)
     g.sync.dma_start(T.y[:], T.ysb[:]).then_inc(T.sem.st, 16)
     g.sync.wait_ge(T.sem.st, 16)
-    g.wait_ge(T.sem.sent, _bits(feed[k]) + _bits(off[k]))
+    g.wait_ge(T.sem.sent, _bits(feed[k]) + 2 * _bits(off[k]))

from concourse.bass import DstId, RemoteDMATransfer

SIM_CORES = 96
N = 9
CW = 128
XW = 32
W = CW + XW

SCRATCH = {
    "cb": ("dram", [128, CW], "bfloat16"),
    "xb": ("dram", [128, XW], "bfloat16"),
    "blk": ("dram", [128, W], "bfloat16"),
    "relc": ("dram", [128, CW], "bfloat16"),
    "relx": ("dram", [128, XW], "bfloat16"),
    "land": ("sbuf", [128, N * W], "bfloat16"),
    "ysb": ("sbuf", [128, XW], "bfloat16"),
    "ps": ("psum", [128, XW], "float32"),
}
SEMAPHORES = ["ldx", "ldc", "ld", "own", "rx", "rc", "sent", "mm", "cp", "st"] + ["a%d" % k for k in range(N)]


def _bits(m):
    return bin(m).count("1")


def _alternate(m):
    out, i = [0, 0], 0
    for b in range(m.bit_length()):
        if m >> b & 1:
            out[i] |= 1 << b
            i = 1 - i
    return out[0], out[1]


def _route(topo, src, dst):
    a, b, d = topo.chip(src), topo.chip(dst), topo.die(src)
    if a == b:
        return []
    if topo.same_plane(a, b):
        return [("out", a, d), ("in", b, d)]
    links = [("mate", a, d)]
    if not topo.mates(a, b):
        m = [topo.chip(c) for c in range(SIM_CORES) if topo.mates(a, topo.chip(c))][0]
        links += [("out", m, d), ("in", b, d)]
    return links


def _plan(T, topo):
    R = list(T.cores)
    n = len(R)
    group = set(R)
    reach = [[r for r in range(n) if r == k or topo.may_write(R[k], R[r])] for k in range(n)]
    pos = [reach[k].index(k) for k in range(n)]
    far = [[r for r in range(n) if r not in reach[k]] for k in range(n)]

    load = {}

    def add(src, dst):
        for l in _route(topo, src, dst):
            load[l] = load.get(l, 0) + 1

    for k in range(n):
        for r in reach[k]:
            if r != k:
                add(R[k], R[r])

    work = {}
    for k in range(n):
        work[k] = {}
        for c in range(SIM_CORES):
            if topo.chip(c) == topo.chip(R[k]) and c not in group and topo.may_write(c, R[far[k][0]]):
                work[k][c] = []

    todo = []
    for k in range(n):
        for r in far[k]:
            todo.append((0 if topo.mates(topo.chip(R[k]), topo.chip(R[r])) else 1, (r - k) % n, k, r))
    for _, _, k, r in sorted(todo):
        best = None
        for c in sorted(work[k]):
            links = _route(topo, c, R[r])
            sw = [load.get(l, 0) + 1 for l in links if l[0] != "mate"]
            if sw:
                busy = max(sw)
            else:
                busy = 0 if topo.die(c) == topo.die(R[k]) else n * n
            key = (len(work[k][c]), busy, max(load.get(l, 0) + 1 for l in links), c)
            if best is None or key < best:
                best = key
        work[k][best[3]].append(r)
        add(best[3], R[r])

    direct, relay, feed, off = {}, {}, {}, {}
    for k in range(n):
        def rank_of_feed(c):
            short = all(topo.mates(topo.chip(c), topo.chip(R[r])) for r in work[k][c])
            return (-len(work[k][c]), short, topo.die(c) == topo.die(R[k]), c)
        cores = [c for c in sorted(work[k], key=rank_of_feed) if work[k][c]]
        xs = dict((c, work[k][c][:1]) for c in cores)
        for c in cores:
            xs[cores[-1]] = xs[cores[-1]] + work[k][c][1:]
        relay[k] = [(c, work[k][c], xs[c]) for c in cores]
        direct[k] = sorted((r for r in reach[k] if r != k), key=lambda r: (pos[r] - pos[k]) % len(reach[k]))
        off[k] = topo.mask(R[k], R[direct[k][0]])
        feed[k] = topo.mask(R[k], cores[0]) & ~off[k]
    return R, direct, relay, feed, off


def _dst(topo, core):
    rid, pid, _ = topo.addr(core)
    return DstId(rid=rid, pnc=pid)


def _slot(T, k):
    return T.land[:, k * W:(k + 1) * W]


def _cpart(T, k):
    return T.land[:, k * W:k * W + CW]


def _xpart(T, k):
    return T.land[:, k * W + CW:(k + 1) * W]


def rank_program(g, core, T, topo):
    R, direct, relay, feed, off = _plan(T, topo)
    n = len(R)
    rank = T.rank_of(core)

    if rank is None:
        for k in range(n):
            for c, rs, xs in relay[k]:
                if c != core:
                    continue
                halves = _alternate(topo.mask(core, R[rs[0]]))
                g.wait_ge(T.sem.rx, _bits(off[k]))
                g.remote_dma_fused([RemoteDMATransfer(
                    dst_ids=[_dst(topo, R[r]) for r in xs], dma_engine_mask=halves[1], remote_sem=T.sem["a%d" % k],
                    srcs=[T.relx[:]], dsts=[_xpart(T, k) for _ in xs])], local_sem=T.sem.sent)
                g.wait_ge(T.sem.rc, _bits(feed[k]))
                g.remote_dma_fused([RemoteDMATransfer(
                    dst_ids=[_dst(topo, R[r])], dma_engine_mask=halves[i], remote_sem=T.sem["a%d" % k],
                    srcs=[T.relc[:]], dsts=[_cpart(T, k)]) for i, r in enumerate(rs)], local_sem=T.sem.sent)
                g.wait_ge(T.sem.sent, _bits(halves[1]) + sum(_bits(halves[i]) for i in range(len(rs))))
        return

    k = rank
    g.scalar.dma_start(T.xb[:], T.x[:]).then_inc(T.sem.ldx, 16)
    g.sync.dma_start(T.cb[:], T.c[:]).then_inc(T.sem.ldc, 16)
    g.sync.dma_start(T.blk[:, 0:CW], T.c[:]).then_inc(T.sem.ld, 16)
    g.scalar.dma_start(T.blk[:, CW:W], T.x[:]).then_inc(T.sem.ld, 16)
    g.sync.dma_start(_cpart(T, k), T.c[:]).then_inc(T.sem.own, 16)
    g.scalar.dma_start(_xpart(T, k), T.x[:]).then_inc(T.sem.own, 16)

    g.wait_ge(T.sem.ldx, 16)
    g.remote_dma_fused([RemoteDMATransfer(
        dst_ids=[_dst(topo, e[0]) for e in relay[k]], dma_engine_mask=off[k], remote_sem=T.sem.rx,
        srcs=[T.xb[:]], dsts=[T.relx[:] for _ in relay[k]])], local_sem=T.sem.sent)
    g.wait_ge(T.sem.ldc, 16)
    g.remote_dma_fused([RemoteDMATransfer(
        dst_ids=[_dst(topo, e[0]) for e in relay[k]], dma_engine_mask=feed[k], remote_sem=T.sem.rc,
        srcs=[T.cb[:]], dsts=[T.relc[:] for _ in relay[k]])], local_sem=T.sem.sent)
    g.wait_ge(T.sem.ld, 32)
    g.remote_dma_fused([RemoteDMATransfer(
        dst_ids=[_dst(topo, R[r]) for r in direct[k]], dma_engine_mask=off[k], remote_sem=T.sem["a%d" % k],
        srcs=[T.blk[:]], dsts=[_slot(T, k) for _ in direct[k]])], local_sem=T.sem.sent)

    due, cnt = {k: 0}, {}
    for s in range(n):
        if s == k:
            continue
        if k in direct[s]:
            due[s] = 1 + direct[s].index(k)
            cnt[s] = _bits(off[s])
        else:
            cnt[s] = 0
            for i, (c, rs, xs) in enumerate(relay[s]):
                halves = _alternate(topo.mask(c, core))
                if k in rs:
                    due[s] = 100 + i + 4 * rs.index(k)
                    cnt[s] += _bits(halves[rs.index(k)])
                if k in xs:
                    cnt[s] += _bits(halves[1])

    order = sorted(range(n), key=lambda a: (max(due[a], due[(k - a) % n]), a))
    seen = set([k])
    g.tensor.wait_ge(T.sem.own, 32)
    for i, a in enumerate(order):
        j = (k - a) % n
        for s in sorted((a, j), key=lambda s: due[s]):
            if s not in seen:
                seen.add(s)
                g.tensor.wait_ge(T.sem["a%d" % s], cnt[s])
        g.tensor.matmul(T.ps[:], _cpart(T, a), _xpart(T, j), i == 0, i == n - 1).then_inc(T.sem.mm, 1)

    g.vector.wait_ge(T.sem.mm, n)
    g.vector.tensor_copy(T.ysb[:], T.ps[:]).then_inc(T.sem.cp, 1)
    g.sync.wait_ge(T.sem.cp, 1)
    g.sync.dma_start(T.y[:], T.ysb[:]).then_inc(T.sem.st, 16)
    g.sync.wait_ge(T.sem.st, 16)
    g.wait_ge(T.sem.sent, _bits(feed[k]) + 2 * _bits(off[k]))
